import numpy as np
import ml_dtypes


def mxq(x, axis, fmt="e4m3"):
    dtype, down = {"e4m3": (ml_dtypes.float8_e4m3fn, 7), "e5m2": (ml_dtypes.float8_e5m2, 14)}[fmt]
    v = np.moveaxis(np.asarray(x, np.float32).astype(ml_dtypes.bfloat16).astype(np.float64), axis, -1)
    blocks = v.reshape(v.shape[:-1] + (-1, 32))
    amax = np.abs(blocks).max(-1, keepdims=True)
    byte = np.maximum(np.where(amax > 0, np.frexp(amax)[1] - 1 + 127, 0) - down, 1)
    scale = np.exp2(byte - 127.0)
    codes = (blocks / scale).astype(np.float32).astype(dtype).astype(np.float64)
    return np.moveaxis((codes * scale).reshape(v.shape), -1, axis)


WIDE = False


def mx_kscale(k):
    if not WIDE:
        return np.ones(k)
    levels = np.array([10, -10, 5, -5, 0])
    if k % 512:
        return np.exp2(np.random.permutation(np.resize(levels, k // 32))).repeat(32)
    a = np.empty((k // 512, 16))
    for p in range(k // 512):
        a[p, :8] = np.random.permutation(np.resize(levels, 8))
        for g in range(8):
            far = levels[np.abs(levels - a[p, g]) >= 10]
            a[p, g + 8] = far[np.random.randint(len(far))]
    return np.exp2(a.ravel()).repeat(32)


def f64(x):
    return np.asarray(x).astype(np.float64)


def striped(idx):
    return np.tile(idx.reshape(-1, 16).T, (8, 1)).astype(np.uint16)


def unstriped(offs):
    return offs[:16].T.reshape(-1).astype(np.int64)


E2M1 = np.array([0.0, 0.5, 1.0, 1.5, 2.0, 3.0, 4.0, 6.0, -0.0, -0.5, -1.0, -1.5, -2.0, -3.0, -4.0, -6.0])


def pack_weight(w, fmt):
    k, n = w.shape
    w = f64(np.asarray(w, np.float32).astype(ml_dtypes.bfloat16)).reshape(k // 32, 32, n)
    amax = np.abs(w).max(1)
    if fmt == "e4m3":
        byte = np.frexp(amax)[1] - 1 + 127 - 7
    else:
        mant, ex = np.frexp(amax / 6.0)
        byte = np.where(mant > 0.5, ex, ex - 1) + 127
    byte = np.clip(np.where(amax > 0, byte, 1), 1, 254)
    scaled = (w * np.exp2(127.0 - byte)[:, None, :]).reshape(k, n).astype(np.float32)
    by_word = np.ascontiguousarray(scaled.reshape(k // 512, 128, 4, n).transpose(0, 1, 3, 2))
    if fmt == "e4m3":
        words = by_word.astype(ml_dtypes.float8_e4m3fn).view(np.uint8)
    else:
        c = by_word.astype(ml_dtypes.float4_e2m1fn).view(np.uint8) & 0xF
        words = (c[..., 0::2] | (c[..., 1::2] << 4)).reshape(k // 512, 128, 2 * n)
    return np.ascontiguousarray(words), np.ascontiguousarray(byte.astype(np.uint8).reshape(k // 512, 16, n))


def unpack_weight(words, scales, fmt):
    g, _, n = scales.shape
    words = np.ascontiguousarray(words).reshape(g, 128, n, -1)
    if fmt == "e4m3":
        vals = words.view(ml_dtypes.float8_e4m3fn).astype(np.float64)
    else:
        nib = np.empty((g, 128, n, 4), np.uint8)
        nib[..., 0::2] = words & 0xF
        nib[..., 1::2] = words >> 4
        vals = E2M1[nib]
    vals = vals * np.repeat(np.exp2(scales.astype(np.float64) - 127.0), 8, axis=1)[..., None]
    return vals.transpose(0, 1, 3, 2).reshape(g * 512, n)


def gelu(v):
    return 0.5 * v * (1.0 + np.tanh(np.sqrt(2.0 / np.pi) * (v + 0.044715 * v**3)))


K, T, S, H, P = 512, 4096, 1024, 1024, 512

def setup_inputs():
    n = np.random.standard_normal
    s = mx_kscale(K)[:, None]
    u = mx_kscale(H)[:, None]
    tab_words, tab_scales = pack_weight(n((K, T)) * s, "e4m3")
    w4_words, w4_scales = pack_weight(1.3 * n((K, H)) / K ** 0.5 / s, "e2m1")
    return {
        "tab_words": tab_words, "tab_scales": tab_scales,
        "offs": striped(np.random.permutation(T)[:S]),
        "w1": (1.3 * n((K, H)) / K ** 0.5 / s).astype(np.float32),
        "w4_words": w4_words, "w4_scales": w4_scales,
        "gain": (np.exp(0.4 * n(H)) * u[:, 0]).astype(np.float32),
        "pos1": striped(np.random.permutation(S)[:P]),
        "w2": (1.4 * n((H, H)) / H ** 0.5 / u).astype(np.float32),
        "absorb": np.exp(0.4 * n((H, P))).astype(np.float32),
        "skip": (np.exp(0.3 * n(H)) / u[:, 0]).astype(np.float32),
        "wgo": np.exp(0.3 * n((128, P))).astype(np.float32),
    }

def reference(tab_words, tab_scales, offs, w1, w4_words, w4_scales, gain, pos1, w2, absorb, skip, wgo):
    v = unpack_weight(tab_words, tab_scales, "e4m3")[:, unstriped(offs)]
    w4 = unpack_weight(w4_words, w4_scales, "e2m1")
    drift = np.tanh(mxq(f64(w1), 0, "e4m3").T @ v)
    near = np.exp(-np.abs(w4.T @ v))
    h = f64(gain)[:, None] * (drift + near)
    x = mxq(h[:, unstriped(pos1)], 0, "e4m3")
    y = np.tanh(mxq(f64(w2), 0, "e4m3").T @ x) * f64(absorb)
    out = f64(skip)[:, None] * h
    out[:, unstriped(pos1)] = np.tile(f64(wgo), (H // 128, 1)) * y
    return out

@@ -1,0 +1,198 @@
+from contextlib import ExitStack
+
+import concourse.mybir as mybir
+
+K, T, S, H, M = 512, 4096, 1024, 1024, 512
+FLOPS = 2 * K * H * S * 2 + 2 * H * H * M
+
+F32 = mybir.dt.float32
+BF16 = mybir.dt.bfloat16
+I32 = mybir.dt.int32
+U32 = mybir.dt.uint32
+U16 = mybir.dt.uint16
+U8 = mybir.dt.uint8
+FP8X4 = mybir.dt.float8_e4m3fn_x4
+FP4X4 = mybir.dt.float4_e2m1fn_x4
+ACT = mybir.ActivationFunctionType
+MULT = mybir.AluOpType.mult
+ADD = mybir.AluOpType.add
+
+P = 128
+PACK = 4
+PASS = P * PACK
+GROUPS = H // PASS
+BANK = 512
+
+
+def tile_list_nozzle_strip_features_kernel(
+    tc, tab_words, tab_scales, offs, w1, w4_words, w4_scales, gain, pos1, w2, absorb, skip, wgo, out
+):
+    nc = tc.nc
+    with ExitStack() as ctx:
+        keep = ctx.enter_context(tc.tile_pool(name="keep", bufs=1))
+        ring = ctx.enter_context(tc.tile_pool(name="ring", bufs=2))
+        psum = ctx.enter_context(tc.psum_pool(name="psum", bufs=8))
+
+        offs_sb = keep.tile([P, S // 16], U16, name="offs_sb")
+        pos_sb = keep.tile([P, M // 16], U16, name="pos_sb")
+        tab_w = keep.tile([P, T], I32, name="tab_w", align_bytes=64)
+        tab_s = keep.tile([P, T // 4], I32, name="tab_s", align_bytes=64)
+        w4_w = keep.tile([P, 2 * H // 4], I32, name="w4_w", align_bytes=64)
+        w4_s = keep.tile([P, H // 4], I32, name="w4_s", align_bytes=64)
+
+        nc.vector.memset(tab_s[:, : T // 8], 0)
+        nc.gpsimd.memset(tab_s[:, T // 8 :], 0)
+        nc.vector.memset(w4_s[:], 0)
+
+        nc.sync.dma_start(offs_sb[:], offs)
+        nc.sync.dma_start(out=w4_w[:], in_=w4_words[0].bitcast(I32))
+        for q in range(4):
+            nc.sync.dma_start(out=tab_s[32 * q : 32 * q + 4, :], in_=tab_scales[0, 4 * q : 4 * q + 4, :].bitcast(I32))
+        nc.sync.dma_start(out=tab_w[:], in_=tab_words[0].rearrange("p t i -> p (t i)").bitcast(I32))
+        for q in range(4):
+            nc.sync.dma_start(out=w4_s[32 * q : 32 * q + 4, :], in_=w4_scales[0, 4 * q : 4 * q + 4, :].bitcast(I32))
+
+        def load_rows(name, rows):
+            raw = keep.tile([P, PACK, PASS], F32, name=name)
+            nc.sync.dma_start(out=raw[:], in_=rows.rearrange("(p j) c -> p j c", j=PACK))
+            return raw
+
+        w1_raw = [load_rows("w1_raw%d" % g, w1[:, PASS * g : PASS * (g + 1)]) for g in range(GROUPS)]
+        nc.sync.dma_start(pos_sb[:], pos1)
+        gain_sb = keep.tile([P, GROUPS, PACK], F32, name="gain_sb")
+        skip_sb = keep.tile([P, GROUPS, PACK], F32, name="skip_sb")
+        nc.sync.dma_start(out=gain_sb[:], in_=gain.rearrange("(g p t) -> p g t", g=GROUPS, t=PACK))
+        nc.sync.dma_start(out=skip_sb[:], in_=skip.rearrange("(g p t) -> p g t", g=GROUPS, t=PACK))
+        w2_raw = {}
+        for g in range(GROUPS):
+            for a in range(GROUPS):
+                w2_raw[a, g] = load_rows(
+                    "w2_raw%d%d" % (a, g), w2[PASS * a : PASS * (a + 1), PASS * g : PASS * (g + 1)]
+                )
+        wgo_sb = keep.tile([P, PACK, M], F32, name="wgo_sb")
+        for q in range(4):
+            nc.sync.dma_start(out=wgo_sb[32 * q : 32 * (q + 1)], in_=wgo.rearrange("(r t) m -> r t m", t=PACK))
+        absorb_sb = [load_rows("absorb%d" % g, absorb[PASS * g : PASS * (g + 1), :]) for g in range(GROUPS)]
+
+        w4_wd = keep.tile([P, 2 * H], U8, name="w4_wd", align_bytes=64)
+        w4_sd = keep.tile([P, H], U8, name="w4_sd", align_bytes=64)
+        for g in range(GROUPS):
+            nc.vector.tensor_copy(
+                out=w4_wd[:, 2 * PASS * g : 2 * PASS * (g + 1)].rearrange("p (t m e) -> p t m e", t=PACK, e=2),
+                in_=w4_w[:].bitcast(U8)[:, 2 * PASS * g : 2 * PASS * (g + 1)].rearrange(
+                    "p (m t e) -> p t m e", t=PACK, e=2
+                ),
+            )
+        for g in range(GROUPS):
+            nc.vector.tensor_copy(
+                out=w4_sd[:, PASS * g : PASS * (g + 1)].rearrange("p (t m) -> p t m", t=PACK),
+                in_=w4_s[:].bitcast(U8)[:, PASS * g : PASS * (g + 1)].rearrange("p (m t) -> p t m", t=PACK),
+            )
+
+        v_w, v_s = [], []
+        for half in range(S // BANK):
+            picks = offs_sb[:, 32 * half : 32 * (half + 1)]
+            words = keep.tile([P, BANK], U32, name="v_w%d" % half, align_bytes=64)
+            scales = keep.tile([P, BANK], U8, name="v_s%d" % half, align_bytes=64)
+            nc.vector.tensor_copy(words[:], tab_w[:].bitcast(U32).indirect(picks))
+            nc.vector.tensor_copy(scales[:], tab_s[:].bitcast(U8).indirect(picks))
+            v_w.append(words)
+            v_s.append(scales)
+
+        def round_pair(copy, raw, u):
+            grouped = ring.tile([P, 2 * P * PACK], BF16, name="grouped", bufs=4, align_bytes=64)
+            copy(
+                out=grouped[:].rearrange("p (e m j) -> p m j e", e=2, j=PACK),
+                in_=raw[:].rearrange("p j (m u e) -> p u m j e", u=2, e=2)[:, u],
+            )
+            return grouped
+
+        def quantise(name, grouped, width):
+            codes = keep.tile([P, width], U32, name=name + "_codes", align_bytes=64)
+            scales = keep.tile([P, width], U8, name=name + "_scales", align_bytes=64)
+            nc.vector.quantize_mx(out=codes[:].bitcast(FP8X4), scales=scales[:], in_=grouped)
+            return codes, scales
+
+        gain_skip = keep.tile([P, GROUPS, PACK], F32, name="gain_skip")
+        nc.vector.tensor_tensor(gain_skip[:], gain_sb[:], skip_sb[:], MULT)
+
+        w1_q = {}
+        feats = []
+        x_q = []
+        for g in range(GROUPS):
+            staged = [round_pair(nc.vector.tensor_copy, w1_raw[g], u) for u in range(2)]
+            for u in range(2):
+                w1_q[g, u] = quantise("w1_%d%d" % (g, u), staged[u][:], 2 * P)
+            x_planes = ring.tile([P, PACK, M], BF16, name="x_planes")
+            for t in range(PACK):
+                i = PACK * g + t
+                near = ring.tile([P, S], F32, name="near", tag="row", bufs=4)
+                feat = keep.tile([P, S], F32, name="feat%d" % i)
+                for half in range(S // BANK):
+                    acc = psum.tile([P, BANK], F32, name="acc")
+                    nc.tensor.matmul_mx(
+                        out=acc[:],
+                        lhsT=w4_wd[:, 2 * P * i : 2 * P * (i + 1)].bitcast(FP4X4),
+                        lhsT_scale=w4_sd[:, P * i : P * (i + 1)],
+                        rhs=v_w[half][:].bitcast(FP8X4),
+                        rhs_scale=v_s[half][:],
+                        start=True,
+                        stop=True,
+                    )
+                    nc.scalar.activation(near[:, BANK * half : BANK * (half + 1)], acc[:], ACT.Abs)
+                nc.scalar.activation(near[:], near[:], ACT.Exp, scale=-1.0)
+                codes, scales = w1_q[g, t // 2]
+                cols = slice(P * (t % 2), P * (t % 2 + 1))
+                for half in range(S // BANK):
+                    acc = psum.tile([P, BANK], F32, name="acc")
+                    nc.tensor.matmul_mx(
+                        out=acc[:],
+                        lhsT=codes[:, cols].bitcast(FP8X4),
+                        lhsT_scale=scales[:, cols],
+                        rhs=v_w[half][:].bitcast(FP8X4),
+                        rhs_scale=v_s[half][:],
+                        start=True,
+                        stop=True,
+                    )
+                    nc.scalar.activation(feat[:, BANK * half : BANK * (half + 1)], acc[:], ACT.Tanh)
+                nc.vector.tensor_tensor(feat[:], feat[:], near[:], ADD)
+                picked = ring.tile([P, M], F32, name="picked")
+                nc.vector.tensor_copy(picked[:], feat[:].indirect(pos_sb[:]))
+                nc.vector.tensor_scalar(x_planes[:, t, :], picked[:], gain_sb[:, g, t : t + 1], None, MULT)
+                feats.append(feat)
+            x_grouped = ring.tile([P, M * PACK], BF16, name="x_grouped", align_bytes=64)
+            nc.vector.tensor_copy(
+                out=x_grouped[:].rearrange("p (c i t) -> p c t i", i=4, t=PACK),
+                in_=x_planes[:].rearrange("p t (c i) -> p c t i", i=4),
+            )
+            x_q.append(quantise("x%d" % g, x_grouped[:], M))
+
+        out_rows = out.rearrange("(g p t) j -> g t p j", g=GROUPS, t=PACK)
+        for g in range(GROUPS):
+            for u in range(2):
+                copy = nc.vector.tensor_copy if (g, u) == (0, 0) else nc.scalar.copy
+                staged = [round_pair(copy, w2_raw[a, g], u) for a in range(GROUPS)]
+                w2_q = [quantise("w2_%d%d%d" % (a, g, u), staged[a][:], 2 * P) for a in range(GROUPS)]
+                for e in range(2):
+                    t = 2 * u + e
+                    i = PACK * g + t
+                    cols = slice(P * e, P * (e + 1))
+                    acc = psum.tile([P, BANK], F32, name="acc")
+                    for a in range(GROUPS):
+                        nc.tensor.matmul_mx(
+                            out=acc[:],
+                            lhsT=w2_q[a][0][:, cols].bitcast(FP8X4),
+                            lhsT_scale=w2_q[a][1][:, cols],
+                            rhs=x_q[a][0][:].bitcast(FP8X4),
+                            rhs_scale=x_q[a][1][:],
+                            start=(a == 0),
+                            stop=(a == GROUPS - 1),
+                        )
+                    page = ring.tile([P, S], F32, name="page", tag="row", bufs=4)
+                    nc.scalar.activation(page[:], feats[i][:], ACT.Copy, scale=gain_skip[:, g, t : t + 1])
+                    worked = ring.tile([P, M], F32, name="worked", bufs=3)
+                    nc.scalar.activation(worked[:], acc[:], ACT.Tanh)
+                    weight = absorb_sb[g][:, t, :]
+                    nc.vector.tensor_tensor(weight, weight, wgo_sb[:, t, :], MULT)
+                    nc.vector.tensor_tensor(page[:].indirect(pos_sb[:]), worked[:], weight, MULT)
+                    nc.sync.dma_start(out=out_rows[g, t], in_=page[:])

@@ -22,6 +22,7 @@ PACK = 4
 PASS = P * PACK
 GROUPS = H // PASS
 BANK = 512
+TILES = GROUPS * PACK
 
 
 def tile_list_nozzle_strip_features_kernel(
@@ -31,14 +32,15 @@ def tile_list_nozzle_strip_features_kernel(
     with ExitStack() as ctx:
         keep = ctx.enter_context(tc.tile_pool(name="keep", bufs=1))
         ring = ctx.enter_context(tc.tile_pool(name="ring", bufs=2))
-        psum = ctx.enter_context(tc.psum_pool(name="psum", bufs=8))
+        arena = ctx.enter_context(tc.tile_pool(name="arena", bufs=1))
+        psum = ctx.enter_context(tc.psum_pool(name="psum", bufs=2))
 
         offs_sb = keep.tile([P, S // 16], U16, name="offs_sb")
         pos_sb = keep.tile([P, M // 16], U16, name="pos_sb")
         tab_w = keep.tile([P, T], I32, name="tab_w", align_bytes=64)
         tab_s = keep.tile([P, T // 4], I32, name="tab_s", align_bytes=64)
         w4_w = keep.tile([P, 2 * H // 4], I32, name="w4_w", align_bytes=64)
-        w4_s = keep.tile([P, H // 4], I32, name="w4_s", align_bytes=64)
+        w4_s = arena.tile([P, H // 4], I32, name="w4_s", offset=1024 * 28, align_bytes=64)
 
         nc.vector.memset(tab_s[:, : T // 8], 0)
         nc.gpsimd.memset(tab_s[:, T // 8 :], 0)
@@ -52,27 +54,28 @@ def tile_list_nozzle_strip_features_kernel(
         for q in range(4):
             nc.sync.dma_start(out=w4_s[32 * q : 32 * q + 4, :], in_=w4_scales[0, 4 * q : 4 * q + 4, :].bitcast(I32))
 
-        def load_rows(name, rows):
-            raw = keep.tile([P, PACK, PASS], F32, name=name)
+        def load_rows(pool, tag, rows):
+            raw = pool.tile([P, PACK, PASS], F32, name=tag)
             nc.sync.dma_start(out=raw[:], in_=rows.rearrange("(p j) c -> p j c", j=PACK))
             return raw
 
-        w1_raw = [load_rows("w1_raw%d" % g, w1[:, PASS * g : PASS * (g + 1)]) for g in range(GROUPS)]
+        def block(w, a, g):
+            return w[PASS * a : PASS * (a + 1), PASS * g : PASS * (g + 1)]
+
+        w1_raw = [load_rows(ring, "w_raw", block(w1, 0, g)) for g in range(GROUPS)]
         nc.sync.dma_start(pos_sb[:], pos1)
         gain_sb = keep.tile([P, GROUPS, PACK], F32, name="gain_sb")
         skip_sb = keep.tile([P, GROUPS, PACK], F32, name="skip_sb")
         nc.sync.dma_start(out=gain_sb[:], in_=gain.rearrange("(g p t) -> p g t", g=GROUPS, t=PACK))
         nc.sync.dma_start(out=skip_sb[:], in_=skip.rearrange("(g p t) -> p g t", g=GROUPS, t=PACK))
-        w2_raw = {}
-        for g in range(GROUPS):
-            for a in range(GROUPS):
-                w2_raw[a, g] = load_rows(
-                    "w2_raw%d%d" % (a, g), w2[PASS * a : PASS * (a + 1), PASS * g : PASS * (g + 1)]
-                )
         wgo_sb = keep.tile([P, PACK, M], F32, name="wgo_sb")
         for q in range(4):
             nc.sync.dma_start(out=wgo_sb[32 * q : 32 * (q + 1)], in_=wgo.rearrange("(r t) m -> r t m", t=PACK))
-        absorb_sb = [load_rows("absorb%d" % g, absorb[PASS * g : PASS * (g + 1), :]) for g in range(GROUPS)]
+        absorb_sb = [load_rows(keep, "absorb0", block(absorb, 0, 0))]
+        w2_raw = {}
+        for a in range(GROUPS):
+            w2_raw[a, 0] = load_rows(keep, "w2_raw%d" % a, block(w2, a, 0))
+        absorb_sb.append(load_rows(keep, "absorb1", block(absorb, 1, 0)))
 
         w4_wd = keep.tile([P, 2 * H], U8, name="w4_wd", align_bytes=64)
         w4_sd = keep.tile([P, H], U8, name="w4_sd", align_bytes=64)
@@ -83,24 +86,30 @@ def tile_list_nozzle_strip_features_kernel(
                     "p (m t e) -> p t m e", t=PACK, e=2
                 ),
             )
-        for g in range(GROUPS):
+
+        def deal_scales(g):
             nc.vector.tensor_copy(
                 out=w4_sd[:, PASS * g : PASS * (g + 1)].rearrange("p (t m) -> p t m", t=PACK),
                 in_=w4_s[:].bitcast(U8)[:, PASS * g : PASS * (g + 1)].rearrange("p (m t) -> p t m", t=PACK),
             )
 
+        deal_scales(0)
+        deal_scales(1)
+
         v_w, v_s = [], []
         for half in range(S // BANK):
             picks = offs_sb[:, 32 * half : 32 * (half + 1)]
-            words = keep.tile([P, BANK], U32, name="v_w%d" % half, align_bytes=64)
+            words = arena.tile([P, BANK], U32, name="v_w%d" % half, offset=1024 * (30, 28)[half], align_bytes=64)
             scales = keep.tile([P, BANK], U8, name="v_s%d" % half, align_bytes=64)
             nc.vector.tensor_copy(words[:], tab_w[:].bitcast(U32).indirect(picks))
             nc.vector.tensor_copy(scales[:], tab_s[:].bitcast(U8).indirect(picks))
             v_w.append(words)
             v_s.append(scales)
 
-        def round_pair(copy, raw, u):
-            grouped = ring.tile([P, 2 * P * PACK], BF16, name="grouped", bufs=4, align_bytes=64)
+        def placed(name, shape, dtype, kib):
+            return arena.tile(shape, dtype, name=name, offset=1024 * kib, align_bytes=64)
+
+        def round_pair(copy, grouped, raw, u):
             copy(
                 out=grouped[:].rearrange("p (e m j) -> p m j e", e=2, j=PACK),
                 in_=raw[:].rearrange("p j (m u e) -> p u m j e", u=2, e=2)[:, u],
@@ -116,83 +125,156 @@ def tile_list_nozzle_strip_features_kernel(
         gain_skip = keep.tile([P, GROUPS, PACK], F32, name="gain_skip")
         nc.vector.tensor_tensor(gain_skip[:], gain_sb[:], skip_sb[:], MULT)
 
+        def pieces_of(width, count):
+            return [slice(width // count * k, width // count * (k + 1)) for k in range(count)]
+
+        def entries(ms):
+            return pos_sb[:, ms.start // 16 : ms.stop // 16]
+
+        rows = [keep.tile([P, PACK * S], F32, name="rows%d" % g) for g in range(GROUPS)]
+
+        def row(r):
+            return rows[r // PACK][:, S * (r % PACK) : S * (r % PACK + 1)]
+
+        def planes(g):
+            return rows[g][:].bitcast(BF16).rearrange("p (t x) -> p t x", t=PACK)[:, :, :M]
+
+        def round_picked(i, picked, ms=slice(0, M)):
+            g, t = divmod(i, PACK)
+            if True:
+                nc.vector.tensor_scalar(planes(g)[:, t, ms], picked[:, ms], gain_sb[:, g, t : t + 1], None, MULT)
+
+        def first_stage(i):
+            g, t = divmod(i, PACK)
+            count = 2 if i == TILES - 1 else 1
+            if i < TILES - 1:
+                home = row((i - 1) % (TILES - 1))
+                near = [home]
+            else:
+                home = row(i)
+                near = [placed("near7a", [P, BANK], F32, 3)[:], home[:, BANK:]]
+            feat = keep.tile([P, S], F32, name="feat%d" % i)
+            for half in range(S // BANK):
+                acc = psum.tile([P, BANK], F32, name="acc_near%d" % half)
+                nc.tensor.matmul_mx(
+                    out=acc[:],
+                    lhsT=w4_wd[:, 2 * P * i : 2 * P * (i + 1)].bitcast(FP4X4),
+                    lhsT_scale=w4_sd[:, P * i : P * (i + 1)],
+                    rhs=v_w[half][:].bitcast(FP8X4),
+                    rhs_scale=v_s[half][:],
+                    start=True,
+                    stop=True,
+                )
+                target = near[half] if count == 2 else near[0][:, BANK * half : BANK * (half + 1)]
+                nc.scalar.activation(target, acc[:], ACT.Abs)
+            for piece in near:
+                nc.scalar.activation(piece, piece, ACT.Exp, scale=-1.0)
+            codes, scales = w1_q[g, t // 2]
+            cols = slice(P * (t % 2), P * (t % 2 + 1))
+            for half in range(S // BANK):
+                acc = psum.tile([P, BANK], F32, name="acc_drift")
+                nc.tensor.matmul_mx(
+                    out=acc[:],
+                    lhsT=codes[:, cols].bitcast(FP8X4),
+                    lhsT_scale=scales[:, cols],
+                    rhs=v_w[half][:].bitcast(FP8X4),
+                    rhs_scale=v_s[half][:],
+                    start=True,
+                    stop=True,
+                )
+                nc.scalar.activation(feat[:, BANK * half : BANK * (half + 1)], acc[:], ACT.Tanh)
+            for js, piece in zip(pieces_of(S, count), near):
+                nc.vector.tensor_tensor(feat[:, js], feat[:, js], piece, ADD)
+            if i < TILES - 1:
+                picked = ring.tile([P, M], F32, name="picked", bufs=3)
+            else:
+                picked = placed("picked7", [P, M], F32, 6)
+            if i < TILES - 1:
+                nc.vector.tensor_copy(picked[:], feat[:].indirect(pos_sb[:]))
+            weight = home[:, S - M :]
+            nc.gpsimd.tensor_tensor(weight, absorb_sb[g][:, t, :], wgo_sb[:, t, :], MULT)
+            return feat, weight, picked
+
+        def quantise_picked(g):
+            x_codes = keep.tile([P, M], U32, name="x_codes%d" % g, align_bytes=64)
+            x_scales = keep.tile([P, M], U8, name="x_scales%d" % g, align_bytes=64)
+            for k, ms in enumerate(pieces_of(M, 2)):
+                if g == 1:
+                    feat, picked = feats[TILES - 1][0], feats[TILES - 1][2]
+                    nc.vector.tensor_copy(picked[:, ms], feat[:].indirect(entries(ms)))
+                    round_picked(TILES - 1, picked, ms)
+                    x_grouped = placed("x_grouped1%d" % k, [P, M // 2 * PACK], BF16, 8 + 4 * k)
+                else:
+                    x_grouped = ring.tile([P, M // 2 * PACK], BF16, name="x_grouped", align_bytes=64)
+                nc.vector.tensor_copy(
+                    out=x_grouped[:].rearrange("p (c i t) -> p c t i", i=4, t=PACK),
+                    in_=planes(g)[:, :, ms].rearrange("p t (c i) -> p c t i", i=4),
+                )
+                nc.vector.quantize_mx(out=x_codes[:, ms].bitcast(FP8X4), scales=x_scales[:, ms], in_=x_grouped[:])
+            return x_codes, x_scales
+
+        def vector_stage(tag, bufs):
+            return ring.tile([P, 2 * P * PACK], BF16, name=tag, bufs=bufs, align_bytes=64)
+
         w1_q = {}
         feats = []
         x_q = []
-        for g in range(GROUPS):
-            staged = [round_pair(nc.vector.tensor_copy, w1_raw[g], u) for u in range(2)]
-            for u in range(2):
-                w1_q[g, u] = quantise("w1_%d%d" % (g, u), staged[u][:], 2 * P)
-            x_planes = ring.tile([P, PACK, M], BF16, name="x_planes")
-            for t in range(PACK):
-                i = PACK * g + t
-                near = ring.tile([P, S], F32, name="near", tag="row", bufs=4)
-                feat = keep.tile([P, S], F32, name="feat%d" % i)
-                for half in range(S // BANK):
-                    acc = psum.tile([P, BANK], F32, name="acc")
-                    nc.tensor.matmul_mx(
-                        out=acc[:],
-                        lhsT=w4_wd[:, 2 * P * i : 2 * P * (i + 1)].bitcast(FP4X4),
-                        lhsT_scale=w4_sd[:, P * i : P * (i + 1)],
-                        rhs=v_w[half][:].bitcast(FP8X4),
-                        rhs_scale=v_s[half][:],
-                        start=True,
-                        stop=True,
-                    )
-                    nc.scalar.activation(near[:, BANK * half : BANK * (half + 1)], acc[:], ACT.Abs)
-                nc.scalar.activation(near[:], near[:], ACT.Exp, scale=-1.0)
-                codes, scales = w1_q[g, t // 2]
-                cols = slice(P * (t % 2), P * (t % 2 + 1))
-                for half in range(S // BANK):
-                    acc = psum.tile([P, BANK], F32, name="acc")
+        for i in range(TILES):
+            if i % 2 == 0:
+                g, u = divmod(i // 2, 2)
+                staged = round_pair(nc.vector.tensor_copy, vector_stage("w1_stage", 2), w1_raw[g], u)
+                w1_q[g, u] = quantise("w1_%d%d" % (g, u), staged[:], 2 * P)
+            if i == TILES - 1:
+                round_picked(i - 1, feats[i - 1][2])
+            feats.append(first_stage(i))
+            if 0 < i < TILES - 1:
+                round_picked(i - 1, feats[i - 1][2])
+            if i == PACK:
+                x_q.append(quantise_picked(0))
+        x_q.append(quantise_picked(1))
+        for a in range(GROUPS):
+            w2_raw[a, 1] = load_rows(ring, "w_raw", block(w2, a, 1))
+
+        def quantise_w2(pair):
+            g, u = divmod(pair, 2)
+            staged = []
+            for a in range(GROUPS):
+                if pair == 0:
+                    staged.append(round_pair(nc.vector.tensor_copy, vector_stage("w2_stage", 2), w2_raw[a, g], u))
+                else:
+                    grouped = placed("by_scalar%d%d" % (pair, a), [P, 2 * P * PACK], BF16, (4, 20, 24)[pair - 1] + 2 * a)
+                    staged.append(round_pair(nc.scalar.copy, grouped, w2_raw[a, g], u))
+            return [quantise("w2_%d%d" % (a, pair), staged[a][:], 2 * P) for a in range(GROUPS)]
+
+        out_rows = out.rearrange("(g p t) j -> g t p j", g=GROUPS, t=PACK)
+        w2_q = [quantise_w2(0)]
+        for i in range(TILES):
+            g, t = divmod(i, PACK)
+            feat, weight = feats[i][:2]
+            cols = slice(P * (i % 2), P * (i % 2 + 1))
+            page = placed("page%d" % i, [P, S], F32, 4 * (0, 2, 3, 4)[i % 4])
+            nc.scalar.activation(page[:], feat[:], ACT.Copy, scale=gain_skip[:, g, t : t + 1])
+            if i == 0:
+                w2_q.append(quantise_w2(1))
+            if i < 3:
+                worked = placed("worked%d" % i, [P, M], F32, (21, 16, 25)[i])
+            else:
+                worked = ring.tile([P, M], F32, name="worked", bufs=3)
+            for ms in pieces_of(M, 2 if i == 0 else 1):
+                acc = psum.tile([P, ms.stop - ms.start], F32, name="acc_worked")
+                for a in range(GROUPS):
+                    codes, scales = w2_q[i // 2][a]
                     nc.tensor.matmul_mx(
                         out=acc[:],
                         lhsT=codes[:, cols].bitcast(FP8X4),
                         lhsT_scale=scales[:, cols],
-                        rhs=v_w[half][:].bitcast(FP8X4),
-                        rhs_scale=v_s[half][:],
-                        start=True,
-                        stop=True,
+                        rhs=x_q[a][0][:, ms].bitcast(FP8X4),
+                        rhs_scale=x_q[a][1][:, ms],
+                        start=(a == 0),
+                        stop=(a == GROUPS - 1),
                     )
-                    nc.scalar.activation(feat[:, BANK * half : BANK * (half + 1)], acc[:], ACT.Tanh)
-                nc.vector.tensor_tensor(feat[:], feat[:], near[:], ADD)
-                picked = ring.tile([P, M], F32, name="picked")
-                nc.vector.tensor_copy(picked[:], feat[:].indirect(pos_sb[:]))
-                nc.vector.tensor_scalar(x_planes[:, t, :], picked[:], gain_sb[:, g, t : t + 1], None, MULT)
-                feats.append(feat)
-            x_grouped = ring.tile([P, M * PACK], BF16, name="x_grouped", align_bytes=64)
-            nc.vector.tensor_copy(
-                out=x_grouped[:].rearrange("p (c i t) -> p c t i", i=4, t=PACK),
-                in_=x_planes[:].rearrange("p t (c i) -> p c t i", i=4),
-            )
-            x_q.append(quantise("x%d" % g, x_grouped[:], M))
-
-        out_rows = out.rearrange("(g p t) j -> g t p j", g=GROUPS, t=PACK)
-        for g in range(GROUPS):
-            for u in range(2):
-                copy = nc.vector.tensor_copy if (g, u) == (0, 0) else nc.scalar.copy
-                staged = [round_pair(copy, w2_raw[a, g], u) for a in range(GROUPS)]
-                w2_q = [quantise("w2_%d%d%d" % (a, g, u), staged[a][:], 2 * P) for a in range(GROUPS)]
-                for e in range(2):
-                    t = 2 * u + e
-                    i = PACK * g + t
-                    cols = slice(P * e, P * (e + 1))
-                    acc = psum.tile([P, BANK], F32, name="acc")
-                    for a in range(GROUPS):
-                        nc.tensor.matmul_mx(
-                            out=acc[:],
-                            lhsT=w2_q[a][0][:, cols].bitcast(FP8X4),
-                            lhsT_scale=w2_q[a][1][:, cols],
-                            rhs=x_q[a][0][:].bitcast(FP8X4),
-                            rhs_scale=x_q[a][1][:],
-                            start=(a == 0),
-                            stop=(a == GROUPS - 1),
-                        )
-                    page = ring.tile([P, S], F32, name="page", tag="row", bufs=4)
-                    nc.scalar.activation(page[:], feats[i][:], ACT.Copy, scale=gain_skip[:, g, t : t + 1])
-                    worked = ring.tile([P, M], F32, name="worked", bufs=3)
-                    nc.scalar.activation(worked[:], acc[:], ACT.Tanh)
-                    weight = absorb_sb[g][:, t, :]
-                    nc.vector.tensor_tensor(weight, weight, wgo_sb[:, t, :], MULT)
-                    nc.vector.tensor_tensor(page[:].indirect(pos_sb[:]), worked[:], weight, MULT)
-                    nc.sync.dma_start(out=out_rows[g, t], in_=page[:])
+                nc.scalar.activation(worked[:, ms], acc[:], ACT.Tanh)
+                nc.vector.tensor_tensor(page[:].indirect(entries(ms)), worked[:, ms], weight[:, ms], MULT)
+            nc.sync.dma_start(out=out_rows[g, t], in_=page[:])
+            if i in (1, 3):
+                w2_q.append(quantise_w2(i // 2 + 2))

@@ -54,28 +54,31 @@ def tile_list_nozzle_strip_features_kernel(
         for q in range(4):
             nc.sync.dma_start(out=w4_s[32 * q : 32 * q + 4, :], in_=w4_scales[0, 4 * q : 4 * q + 4, :].bitcast(I32))
 
-        def load_rows(pool, tag, rows):
-            raw = pool.tile([P, PACK, PASS], F32, name=tag)
+        def placed(name, shape, dtype, kib):
+            return arena.tile(shape, dtype, name=name, offset=1024 * kib, align_bytes=64)
+
+        def load_rows(name, rows, kib=None):
+            raw = keep.tile([P, PACK, PASS], F32, name=name) if kib is None else placed(name, [P, PACK, PASS], F32, kib)
             nc.sync.dma_start(out=raw[:], in_=rows.rearrange("(p j) c -> p j c", j=PACK))
             return raw
 
         def block(w, a, g):
             return w[PASS * a : PASS * (a + 1), PASS * g : PASS * (g + 1)]
 
-        w1_raw = [load_rows(ring, "w_raw", block(w1, 0, g)) for g in range(GROUPS)]
+        w1_raw = [load_rows("w1_raw%d" % g, block(w1, 0, g), 40 - 8 * g) for g in range(GROUPS)]
         nc.sync.dma_start(pos_sb[:], pos1)
         gain_sb = keep.tile([P, GROUPS, PACK], F32, name="gain_sb")
         skip_sb = keep.tile([P, GROUPS, PACK], F32, name="skip_sb")
         nc.sync.dma_start(out=gain_sb[:], in_=gain.rearrange("(g p t) -> p g t", g=GROUPS, t=PACK))
         nc.sync.dma_start(out=skip_sb[:], in_=skip.rearrange("(g p t) -> p g t", g=GROUPS, t=PACK))
+        w2_raw = {}
+        for a in range(GROUPS):
+            w2_raw[a, 0] = load_rows("w2_raw%d" % a, block(w2, a, 0))
         wgo_sb = keep.tile([P, PACK, M], F32, name="wgo_sb")
         for q in range(4):
             nc.sync.dma_start(out=wgo_sb[32 * q : 32 * (q + 1)], in_=wgo.rearrange("(r t) m -> r t m", t=PACK))
-        absorb_sb = [load_rows(keep, "absorb0", block(absorb, 0, 0))]
-        w2_raw = {}
-        for a in range(GROUPS):
-            w2_raw[a, 0] = load_rows(keep, "w2_raw%d" % a, block(w2, a, 0))
-        absorb_sb.append(load_rows(keep, "absorb1", block(absorb, 1, 0)))
+        absorb_sb = [load_rows("absorb0", block(absorb, 0, 0))]
+        absorb_sb.append(load_rows("absorb1", block(absorb, 1, 0)))
 
         w4_wd = keep.tile([P, 2 * H], U8, name="w4_wd", align_bytes=64)
         w4_sd = keep.tile([P, H], U8, name="w4_sd", align_bytes=64)
@@ -106,19 +109,20 @@ def tile_list_nozzle_strip_features_kernel(
             v_w.append(words)
             v_s.append(scales)
 
-        def placed(name, shape, dtype, kib):
-            return arena.tile(shape, dtype, name=name, offset=1024 * kib, align_bytes=64)
-
         def round_pair(copy, grouped, raw, u):
             copy(
-                out=grouped[:].rearrange("p (e m j) -> p m j e", e=2, j=PACK),
+                out=grouped.rearrange("p (e m j) -> p m j e", e=2, j=PACK),
                 in_=raw[:].rearrange("p j (m u e) -> p u m j e", u=2, e=2)[:, u],
             )
             return grouped
 
-        def quantise(name, grouped, width):
-            codes = keep.tile([P, width], U32, name=name + "_codes", align_bytes=64)
-            scales = keep.tile([P, width], U8, name=name + "_scales", align_bytes=64)
+        def quantise(name, grouped, width, kibs=None):
+            if kibs is None:
+                codes = keep.tile([P, width], U32, name=name + "_codes", align_bytes=64)
+                scales = keep.tile([P, width], U8, name=name + "_scales", align_bytes=64)
+            else:
+                codes = placed(name + "_codes", [P, width], U32, kibs[0])
+                scales = placed(name + "_scales", [P, width], U8, kibs[1])
             nc.vector.quantize_mx(out=codes[:].bitcast(FP8X4), scales=scales[:], in_=grouped)
             return codes, scales
 
@@ -152,7 +156,7 @@ def tile_list_nozzle_strip_features_kernel(
                 near = [home]
             else:
                 home = row(i)
-                near = [placed("near7a", [P, BANK], F32, 3)[:], home[:, BANK:]]
+                near = [home[:, :BANK], home[:, BANK:]]
             feat = keep.tile([P, S], F32, name="feat%d" % i)
             for half in range(S // BANK):
                 acc = psum.tile([P, BANK], F32, name="acc_near%d" % half)
@@ -185,27 +189,23 @@ def tile_list_nozzle_strip_features_kernel(
                 nc.scalar.activation(feat[:, BANK * half : BANK * (half + 1)], acc[:], ACT.Tanh)
             for js, piece in zip(pieces_of(S, count), near):
                 nc.vector.tensor_tensor(feat[:, js], feat[:, js], piece, ADD)
-            if i < TILES - 1:
-                picked = ring.tile([P, M], F32, name="picked", bufs=3)
+            if i == TILES - 2:
+                picked = placed("picked%d" % i, [P, M], F32, 0)
             else:
-                picked = placed("picked7", [P, M], F32, 6)
+                picked = ring.tile([P, M], F32, name="picked", bufs=3)
             if i < TILES - 1:
                 nc.vector.tensor_copy(picked[:], feat[:].indirect(pos_sb[:]))
-            weight = home[:, S - M :]
-            nc.gpsimd.tensor_tensor(weight, absorb_sb[g][:, t, :], wgo_sb[:, t, :], MULT)
-            return feat, weight, picked
+            return feat, picked
 
         def quantise_picked(g):
             x_codes = keep.tile([P, M], U32, name="x_codes%d" % g, align_bytes=64)
             x_scales = keep.tile([P, M], U8, name="x_scales%d" % g, align_bytes=64)
             for k, ms in enumerate(pieces_of(M, 2)):
                 if g == 1:
-                    feat, picked = feats[TILES - 1][0], feats[TILES - 1][2]
+                    feat, picked = feats[TILES - 1]
                     nc.vector.tensor_copy(picked[:, ms], feat[:].indirect(entries(ms)))
                     round_picked(TILES - 1, picked, ms)
-                    x_grouped = placed("x_grouped1%d" % k, [P, M // 2 * PACK], BF16, 8 + 4 * k)
-                else:
-                    x_grouped = ring.tile([P, M // 2 * PACK], BF16, name="x_grouped", align_bytes=64)
+                x_grouped = ring.tile([P, M // 2 * PACK], BF16, name="x_grouped", align_bytes=64)
                 nc.vector.tensor_copy(
                     out=x_grouped[:].rearrange("p (c i t) -> p c t i", i=4, t=PACK),
                     in_=planes(g)[:, :, ms].rearrange("p t (c i) -> p c t i", i=4),
@@ -214,7 +214,7 @@ def tile_list_nozzle_strip_features_kernel(
             return x_codes, x_scales
 
         def vector_stage(tag, bufs):
-            return ring.tile([P, 2 * P * PACK], BF16, name=tag, bufs=bufs, align_bytes=64)
+            return ring.tile([P, 2 * P * PACK], BF16, name=tag, bufs=bufs, align_bytes=64)[:]
 
         w1_q = {}
         feats = []
@@ -223,58 +223,57 @@ def tile_list_nozzle_strip_features_kernel(
             if i % 2 == 0:
                 g, u = divmod(i // 2, 2)
                 staged = round_pair(nc.vector.tensor_copy, vector_stage("w1_stage", 2), w1_raw[g], u)
-                w1_q[g, u] = quantise("w1_%d%d" % (g, u), staged[:], 2 * P)
+                w1_q[g, u] = quantise("w1_%d%d" % (g, u), staged, 2 * P, (20, 4) if i == TILES - 2 else None)
             if i == TILES - 1:
-                round_picked(i - 1, feats[i - 1][2])
+                round_picked(i - 1, feats[i - 1][1])
             feats.append(first_stage(i))
             if 0 < i < TILES - 1:
-                round_picked(i - 1, feats[i - 1][2])
+                round_picked(i - 1, feats[i - 1][1])
             if i == PACK:
                 x_q.append(quantise_picked(0))
         x_q.append(quantise_picked(1))
         for a in range(GROUPS):
-            w2_raw[a, 1] = load_rows(ring, "w_raw", block(w2, a, 1))
+            w2_raw[a, 1] = load_rows("w2_late%d" % a, block(w2, a, 1), 40 - 8 * a)
 
-        def quantise_w2(pair):
-            g, u = divmod(pair, 2)
-            staged = []
-            for a in range(GROUPS):
-                if pair == 0:
-                    staged.append(round_pair(nc.vector.tensor_copy, vector_stage("w2_stage", 2), w2_raw[a, g], u))
-                else:
-                    grouped = placed("by_scalar%d%d" % (pair, a), [P, 2 * P * PACK], BF16, (4, 20, 24)[pair - 1] + 2 * a)
-                    staged.append(round_pair(nc.scalar.copy, grouped, w2_raw[a, g], u))
-            return [quantise("w2_%d%d" % (a, pair), staged[a][:], 2 * P) for a in range(GROUPS)]
+        w2_q = {}
+
+        def quantise_w2(copy, staged, pairs):
+            blocks = [(pair, a) for pair in pairs for a in range(GROUPS)]
+            for n, (pair, a) in enumerate(blocks):
+                g, u = divmod(pair, 2)
+                round_pair(copy, staged[:, 2 * PASS * n : 2 * PASS * (n + 1)], w2_raw[a, g], u)
+            codes, scales = quantise("w2_%d" % pairs[0], staged[:], 2 * P * len(blocks))
+            for n, key in enumerate(blocks):
+                w2_q[key] = (codes[:, 2 * P * n : 2 * P * (n + 1)], scales[:, 2 * P * n : 2 * P * (n + 1)])
 
         out_rows = out.rearrange("(g p t) j -> g t p j", g=GROUPS, t=PACK)
-        w2_q = [quantise_w2(0)]
+        weights = [placed("weight_first", [P, M], F32, 11), placed("weight_rest", [P, M], F32, 12)]
+        quantise_w2(nc.vector.tensor_copy, keep.tile([P, 4 * PASS], BF16, name="w2_first", align_bytes=64), [0])
+        quantise_w2(nc.scalar.copy, placed("w2_second", [P, 4 * PASS], BF16, 4), [1])
+        quantise_w2(nc.scalar.copy, placed("w2_rest", [P, 8 * PASS], BF16, 20), [2, 3])
         for i in range(TILES):
             g, t = divmod(i, PACK)
-            feat, weight = feats[i][:2]
+            feat = feats[i][0]
             cols = slice(P * (i % 2), P * (i % 2 + 1))
-            page = placed("page%d" % i, [P, S], F32, 4 * (0, 2, 3, 4)[i % 4])
+            page = placed("page%d" % i, [P, S], F32, (0, 8, 30, 34)[i % 4])
             nc.scalar.activation(page[:], feat[:], ACT.Copy, scale=gain_skip[:, g, t : t + 1])
-            if i == 0:
-                w2_q.append(quantise_w2(1))
-            if i < 3:
-                worked = placed("worked%d" % i, [P, M], F32, (21, 16, 25)[i])
-            else:
-                worked = ring.tile([P, M], F32, name="worked", bufs=3)
-            for ms in pieces_of(M, 2 if i == 0 else 1):
-                acc = psum.tile([P, ms.stop - ms.start], F32, name="acc_worked")
-                for a in range(GROUPS):
-                    codes, scales = w2_q[i // 2][a]
-                    nc.tensor.matmul_mx(
-                        out=acc[:],
-                        lhsT=codes[:, cols].bitcast(FP8X4),
-                        lhsT_scale=scales[:, cols],
-                        rhs=x_q[a][0][:, ms].bitcast(FP8X4),
-                        rhs_scale=x_q[a][1][:, ms],
-                        start=(a == 0),
-                        stop=(a == GROUPS - 1),
-                    )
-                nc.scalar.activation(worked[:, ms], acc[:], ACT.Tanh)
-                nc.vector.tensor_tensor(page[:].indirect(entries(ms)), worked[:, ms], weight[:, ms], MULT)
+            worked = placed("worked%d" % i, [P, M], F32, (32, 34, 40, 42, 44, 46, 38, 16)[i])
+            acc = psum.tile([P, M], F32, name="acc_worked")
+            for a in range(GROUPS):
+                codes, scales = w2_q[i // 2, a]
+                nc.tensor.matmul_mx(
+                    out=acc[:],
+                    lhsT=codes[:, cols].bitcast(FP8X4),
+                    lhsT_scale=scales[:, cols],
+                    rhs=x_q[a][0][:].bitcast(FP8X4),
+                    rhs_scale=x_q[a][1][:],
+                    start=(a == 0),
+                    stop=(a == GROUPS - 1),
+                )
+            nc.scalar.activation(worked[:], acc[:], ACT.Tanh)
+            engine = nc.vector if i == 0 else nc.gpsimd
+            weight = weights[min(i, 1)]
+            engine.tensor_tensor(weight[:], absorb_sb[g][:, t, :], wgo_sb[:, t, :], MULT)
+            engine.tensor_tensor(worked[:], worked[:], weight[:], MULT)
+            nc.vector.tensor_copy(page[:].indirect(pos_sb[:]), worked[:])
             nc.sync.dma_start(out=out_rows[g, t], in_=page[:])
-            if i in (1, 3):
-                w2_q.append(quantise_w2(i // 2 + 2))

@@ -55,7 +55,7 @@ def tile_list_nozzle_strip_features_kernel(
             nc.sync.dma_start(out=w4_s[32 * q : 32 * q + 4, :], in_=w4_scales[0, 4 * q : 4 * q + 4, :].bitcast(I32))
 
         def placed(name, shape, dtype, kib):
-            return arena.tile(shape, dtype, name=name, offset=1024 * kib, align_bytes=64)
+            return arena.tile(shape, dtype, name=name, offset=int(1024 * kib), align_bytes=64)
 
         def load_rows(name, rows, kib=None):
             raw = keep.tile([P, PACK, PASS], F32, name=name) if kib is None else placed(name, [P, PACK, PASS], F32, kib)
@@ -145,7 +145,9 @@ def tile_list_nozzle_strip_features_kernel(
 
         def round_picked(i, picked, ms=slice(0, M)):
             g, t = divmod(i, PACK)
-            if True:
+            if i < TILES - 2:
+                nc.gpsimd.tensor_scalar(planes(g)[:, t, ms], picked[:, ms], gain_sb[:, g, t : t + 1], 0.0, MULT, ADD)
+            else:
                 nc.vector.tensor_scalar(planes(g)[:, t, ms], picked[:, ms], gain_sb[:, g, t : t + 1], None, MULT)
 
         def first_stage(i):
@@ -189,10 +191,7 @@ def tile_list_nozzle_strip_features_kernel(
                 nc.scalar.activation(feat[:, BANK * half : BANK * (half + 1)], acc[:], ACT.Tanh)
             for js, piece in zip(pieces_of(S, count), near):
                 nc.vector.tensor_tensor(feat[:, js], feat[:, js], piece, ADD)
-            if i == TILES - 2:
-                picked = placed("picked%d" % i, [P, M], F32, 0)
-            else:
-                picked = ring.tile([P, M], F32, name="picked", bufs=3)
+            picked = ring.tile([P, M], F32, name="picked", bufs=3)
             if i < TILES - 1:
                 nc.vector.tensor_copy(picked[:], feat[:].indirect(pos_sb[:]))
             return feat, picked
@@ -223,10 +222,13 @@ def tile_list_nozzle_strip_features_kernel(
             if i % 2 == 0:
                 g, u = divmod(i // 2, 2)
                 staged = round_pair(nc.vector.tensor_copy, vector_stage("w1_stage", 2), w1_raw[g], u)
-                w1_q[g, u] = quantise("w1_%d%d" % (g, u), staged, 2 * P, (20, 4) if i == TILES - 2 else None)
+                w1_q[g, u] = quantise("w1_%d%d" % (g, u), staged, 2 * P, (23.5, 4) if i == TILES - 2 else None)
             if i == TILES - 1:
                 round_picked(i - 1, feats[i - 1][1])
             feats.append(first_stage(i))
+            if i == 0:
+                first_page = placed("page0", [P, S], F32, 0)
+                nc.gpsimd.tensor_scalar(first_page[:], feats[0][0][:], gain_skip[:, 0, 0:1], 0.0, MULT, ADD)
             if 0 < i < TILES - 1:
                 round_picked(i - 1, feats[i - 1][1])
             if i == PACK:
@@ -250,13 +252,17 @@ def tile_list_nozzle_strip_features_kernel(
         weights = [placed("weight_first", [P, M], F32, 11), placed("weight_rest", [P, M], F32, 12)]
         quantise_w2(nc.vector.tensor_copy, keep.tile([P, 4 * PASS], BF16, name="w2_first", align_bytes=64), [0])
         quantise_w2(nc.scalar.copy, placed("w2_second", [P, 4 * PASS], BF16, 4), [1])
-        quantise_w2(nc.scalar.copy, placed("w2_rest", [P, 8 * PASS], BF16, 20), [2, 3])
+        quantise_w2(nc.scalar.copy, placed("w2_third", [P, 4 * PASS], BF16, 20), [2])
+        quantise_w2(nc.scalar.copy, placed("w2_fourth", [P, 4 * PASS], BF16, 24), [3])
         for i in range(TILES):
             g, t = divmod(i, PACK)
             feat = feats[i][0]
             cols = slice(P * (i % 2), P * (i % 2 + 1))
-            page = placed("page%d" % i, [P, S], F32, (0, 8, 30, 34)[i % 4])
-            nc.scalar.activation(page[:], feat[:], ACT.Copy, scale=gain_skip[:, g, t : t + 1])
+            if i == 0:
+                page = first_page
+            else:
+                page = placed("page%d" % i, [P, S], F32, (0, 8, 30, 34)[i % 4])
+                nc.scalar.activation(page[:], feat[:], ACT.Copy, scale=gain_skip[:, g, t : t + 1])
             worked = placed("worked%d" % i, [P, M], F32, (32, 34, 40, 42, 44, 46, 38, 16)[i])
             acc = psum.tile([P, M], F32, name="acc_worked")
             for a in range(GROUPS):

from contextlib import ExitStack

import concourse.mybir as mybir

K, T, S, H, M = 512, 4096, 1024, 1024, 512
FLOPS = 2 * K * H * S * 2 + 2 * H * H * M

F32 = mybir.dt.float32
BF16 = mybir.dt.bfloat16
I32 = mybir.dt.int32
U32 = mybir.dt.uint32
U16 = mybir.dt.uint16
U8 = mybir.dt.uint8
FP8X4 = mybir.dt.float8_e4m3fn_x4
FP4X4 = mybir.dt.float4_e2m1fn_x4
ACT = mybir.ActivationFunctionType
MULT = mybir.AluOpType.mult
ADD = mybir.AluOpType.add

P = 128
PACK = 4
PASS = P * PACK
GROUPS = H // PASS
BANK = 512
TILES = GROUPS * PACK


def tile_list_nozzle_strip_features_kernel(
    tc, tab_words, tab_scales, offs, w1, w4_words, w4_scales, gain, pos1, w2, absorb, skip, wgo, out
):
    nc = tc.nc
    with ExitStack() as ctx:
        keep = ctx.enter_context(tc.tile_pool(name="keep", bufs=1))
        ring = ctx.enter_context(tc.tile_pool(name="ring", bufs=2))
        arena = ctx.enter_context(tc.tile_pool(name="arena", bufs=1))
        psum = ctx.enter_context(tc.psum_pool(name="psum", bufs=2))

        offs_sb = keep.tile([P, S // 16], U16, name="offs_sb")
        pos_sb = keep.tile([P, M // 16], U16, name="pos_sb")
        tab_w = keep.tile([P, T], I32, name="tab_w", align_bytes=64)
        tab_s = keep.tile([P, T // 4], I32, name="tab_s", align_bytes=64)
        w4_w = keep.tile([P, 2 * H // 4], I32, name="w4_w", align_bytes=64)
        w4_s = arena.tile([P, H // 4], I32, name="w4_s", offset=1024 * 28, align_bytes=64)

        nc.vector.memset(tab_s[:, : T // 8], 0)
        nc.gpsimd.memset(tab_s[:, T // 8 :], 0)
        nc.vector.memset(w4_s[:], 0)

        nc.sync.dma_start(offs_sb[:], offs)
        nc.sync.dma_start(out=w4_w[:], in_=w4_words[0].bitcast(I32))
        for q in range(4):
            nc.sync.dma_start(out=tab_s[32 * q : 32 * q + 4, :], in_=tab_scales[0, 4 * q : 4 * q + 4, :].bitcast(I32))
        nc.sync.dma_start(out=tab_w[:], in_=tab_words[0].rearrange("p t i -> p (t i)").bitcast(I32))
        for q in range(4):
            nc.sync.dma_start(out=w4_s[32 * q : 32 * q + 4, :], in_=w4_scales[0, 4 * q : 4 * q + 4, :].bitcast(I32))

        def placed(name, shape, dtype, kib):
            return arena.tile(shape, dtype, name=name, offset=int(1024 * kib), align_bytes=64)

        def load_rows(name, rows, kib=None):
            raw = keep.tile([P, PACK, PASS], F32, name=name) if kib is None else placed(name, [P, PACK, PASS], F32, kib)
            nc.sync.dma_start(out=raw[:], in_=rows.rearrange("(p j) c -> p j c", j=PACK))
            return raw

        def block(w, a, g):
            return w[PASS * a : PASS * (a + 1), PASS * g : PASS * (g + 1)]

        w1_raw = [load_rows("w1_raw%d" % g, block(w1, 0, g), 40 - 8 * g) for g in range(GROUPS)]
        nc.sync.dma_start(pos_sb[:], pos1)
        gain_sb = keep.tile([P, GROUPS, PACK], F32, name="gain_sb")
        skip_sb = keep.tile([P, GROUPS, PACK], F32, name="skip_sb")
        nc.sync.dma_start(out=gain_sb[:], in_=gain.rearrange("(g p t) -> p g t", g=GROUPS, t=PACK))
        nc.sync.dma_start(out=skip_sb[:], in_=skip.rearrange("(g p t) -> p g t", g=GROUPS, t=PACK))
        w2_raw = {}
        for a in range(GROUPS):
            w2_raw[a, 0] = load_rows("w2_raw%d" % a, block(w2, a, 0))
        wgo_sb = keep.tile([P, PACK, M], F32, name="wgo_sb")
        for q in range(4):
            nc.sync.dma_start(out=wgo_sb[32 * q : 32 * (q + 1)], in_=wgo.rearrange("(r t) m -> r t m", t=PACK))
        absorb_sb = [load_rows("absorb0", block(absorb, 0, 0))]
        absorb_sb.append(load_rows("absorb1", block(absorb, 1, 0)))

        w4_wd = keep.tile([P, 2 * H], U8, name="w4_wd", align_bytes=64)
        w4_sd = keep.tile([P, H], U8, name="w4_sd", align_bytes=64)
        for g in range(GROUPS):
            nc.vector.tensor_copy(
                out=w4_wd[:, 2 * PASS * g : 2 * PASS * (g + 1)].rearrange("p (t m e) -> p t m e", t=PACK, e=2),
                in_=w4_w[:].bitcast(U8)[:, 2 * PASS * g : 2 * PASS * (g + 1)].rearrange(
                    "p (m t e) -> p t m e", t=PACK, e=2
                ),
            )

        def deal_scales(g):
            nc.vector.tensor_copy(
                out=w4_sd[:, PASS * g : PASS * (g + 1)].rearrange("p (t m) -> p t m", t=PACK),
                in_=w4_s[:].bitcast(U8)[:, PASS * g : PASS * (g + 1)].rearrange("p (m t) -> p t m", t=PACK),
            )

        deal_scales(0)
        deal_scales(1)

        v_w, v_s = [], []
        for half in range(S // BANK):
            picks = offs_sb[:, 32 * half : 32 * (half + 1)]
            words = arena.tile([P, BANK], U32, name="v_w%d" % half, offset=1024 * (30, 28)[half], align_bytes=64)
            scales = keep.tile([P, BANK], U8, name="v_s%d" % half, align_bytes=64)
            nc.vector.tensor_copy(words[:], tab_w[:].bitcast(U32).indirect(picks))
            nc.vector.tensor_copy(scales[:], tab_s[:].bitcast(U8).indirect(picks))
            v_w.append(words)
            v_s.append(scales)

        def round_pair(copy, grouped, raw, u):
            copy(
                out=grouped.rearrange("p (e m j) -> p m j e", e=2, j=PACK),
                in_=raw[:].rearrange("p j (m u e) -> p u m j e", u=2, e=2)[:, u],
            )
            return grouped

        def quantise(name, grouped, width, kibs=None):
            if kibs is None:
                codes = keep.tile([P, width], U32, name=name + "_codes", align_bytes=64)
                scales = keep.tile([P, width], U8, name=name + "_scales", align_bytes=64)
            else:
                codes = placed(name + "_codes", [P, width], U32, kibs[0])
                scales = placed(name + "_scales", [P, width], U8, kibs[1])
            nc.vector.quantize_mx(out=codes[:].bitcast(FP8X4), scales=scales[:], in_=grouped)
            return codes, scales

        gain_skip = keep.tile([P, GROUPS, PACK], F32, name="gain_skip")
        nc.vector.tensor_tensor(gain_skip[:], gain_sb[:], skip_sb[:], MULT)

        def pieces_of(width, count):
            return [slice(width // count * k, width // count * (k + 1)) for k in range(count)]

        def entries(ms):
            return pos_sb[:, ms.start // 16 : ms.stop // 16]

        rows = [keep.tile([P, PACK * S], F32, name="rows%d" % g) for g in range(GROUPS)]

        def row(r):
            return rows[r // PACK][:, S * (r % PACK) : S * (r % PACK + 1)]

        def planes(g):
            return rows[g][:].bitcast(BF16).rearrange("p (t x) -> p t x", t=PACK)[:, :, :M]

        def round_picked(i, picked, ms=slice(0, M)):
            g, t = divmod(i, PACK)
            if i < TILES - 2:
                nc.gpsimd.tensor_scalar(planes(g)[:, t, ms], picked[:, ms], gain_sb[:, g, t : t + 1], 0.0, MULT, ADD)
            else:
                nc.vector.tensor_scalar(planes(g)[:, t, ms], picked[:, ms], gain_sb[:, g, t : t + 1], None, MULT)

        def first_stage(i):
            g, t = divmod(i, PACK)
            count = 2 if i == TILES - 1 else 1
            if i < TILES - 1:
                home = row((i - 1) % (TILES - 1))
                near = [home]
            else:
                home = row(i)
                near = [home[:, :BANK], home[:, BANK:]]
            feat = keep.tile([P, S], F32, name="feat%d" % i)
            for half in range(S // BANK):
                acc = psum.tile([P, BANK], F32, name="acc_near%d" % half)
                nc.tensor.matmul_mx(
                    out=acc[:],
                    lhsT=w4_wd[:, 2 * P * i : 2 * P * (i + 1)].bitcast(FP4X4),
                    lhsT_scale=w4_sd[:, P * i : P * (i + 1)],
                    rhs=v_w[half][:].bitcast(FP8X4),
                    rhs_scale=v_s[half][:],
                    start=True,
                    stop=True,
                )
                target = near[half] if count == 2 else near[0][:, BANK * half : BANK * (half + 1)]
                nc.scalar.activation(target, acc[:], ACT.Abs)
            for piece in near:
                nc.scalar.activation(piece, piece, ACT.Exp, scale=-1.0)
            codes, scales = w1_q[g, t // 2]
            cols = slice(P * (t % 2), P * (t % 2 + 1))
            for half in range(S // BANK):
                acc = psum.tile([P, BANK], F32, name="acc_drift")
                nc.tensor.matmul_mx(
                    out=acc[:],
                    lhsT=codes[:, cols].bitcast(FP8X4),
                    lhsT_scale=scales[:, cols],
                    rhs=v_w[half][:].bitcast(FP8X4),
                    rhs_scale=v_s[half][:],
                    start=True,
                    stop=True,
                )
                nc.scalar.activation(feat[:, BANK * half : BANK * (half + 1)], acc[:], ACT.Tanh)
            for js, piece in zip(pieces_of(S, count), near):
                nc.vector.tensor_tensor(feat[:, js], feat[:, js], piece, ADD)
            picked = ring.tile([P, M], F32, name="picked", bufs=3)
            if i < TILES - 1:
                nc.vector.tensor_copy(picked[:], feat[:].indirect(pos_sb[:]))
            return feat, picked

        def quantise_picked(g):
            x_codes = keep.tile([P, M], U32, name="x_codes%d" % g, align_bytes=64)
            x_scales = keep.tile([P, M], U8, name="x_scales%d" % g, align_bytes=64)
            for k, ms in enumerate(pieces_of(M, 2)):
                if g == 1:
                    feat, picked = feats[TILES - 1]
                    nc.vector.tensor_copy(picked[:, ms], feat[:].indirect(entries(ms)))
                    round_picked(TILES - 1, picked, ms)
                x_grouped = ring.tile([P, M // 2 * PACK], BF16, name="x_grouped", align_bytes=64)
                nc.vector.tensor_copy(
                    out=x_grouped[:].rearrange("p (c i t) -> p c t i", i=4, t=PACK),
                    in_=planes(g)[:, :, ms].rearrange("p t (c i) -> p c t i", i=4),
                )
                nc.vector.quantize_mx(out=x_codes[:, ms].bitcast(FP8X4), scales=x_scales[:, ms], in_=x_grouped[:])
            return x_codes, x_scales

        def vector_stage(tag, bufs):
            return ring.tile([P, 2 * P * PACK], BF16, name=tag, bufs=bufs, align_bytes=64)[:]

        w1_q = {}
        feats = []
        x_q = []
        for i in range(TILES):
            if i % 2 == 0:
                g, u = divmod(i // 2, 2)
                staged = round_pair(nc.vector.tensor_copy, vector_stage("w1_stage", 2), w1_raw[g], u)
                w1_q[g, u] = quantise("w1_%d%d" % (g, u), staged, 2 * P, (23.5, 4) if i == TILES - 2 else None)
            if i == TILES - 1:
                round_picked(i - 1, feats[i - 1][1])
            feats.append(first_stage(i))
            if i == 0:
                first_page = placed("page0", [P, S], F32, 0)
                nc.gpsimd.tensor_scalar(first_page[:], feats[0][0][:], gain_skip[:, 0, 0:1], 0.0, MULT, ADD)
            if 0 < i < TILES - 1:
                round_picked(i - 1, feats[i - 1][1])
            if i == PACK:
                x_q.append(quantise_picked(0))
        x_q.append(quantise_picked(1))
        for a in range(GROUPS):
            w2_raw[a, 1] = load_rows("w2_late%d" % a, block(w2, a, 1), 40 - 8 * a)

        w2_q = {}

        def quantise_w2(copy, staged, pairs):
            blocks = [(pair, a) for pair in pairs for a in range(GROUPS)]
            for n, (pair, a) in enumerate(blocks):
                g, u = divmod(pair, 2)
                round_pair(copy, staged[:, 2 * PASS * n : 2 * PASS * (n + 1)], w2_raw[a, g], u)
            codes, scales = quantise("w2_%d" % pairs[0], staged[:], 2 * P * len(blocks))
            for n, key in enumerate(blocks):
                w2_q[key] = (codes[:, 2 * P * n : 2 * P * (n + 1)], scales[:, 2 * P * n : 2 * P * (n + 1)])

        out_rows = out.rearrange("(g p t) j -> g t p j", g=GROUPS, t=PACK)
        weights = [placed("weight_first", [P, M], F32, 11), placed("weight_rest", [P, M], F32, 12)]
        quantise_w2(nc.vector.tensor_copy, keep.tile([P, 4 * PASS], BF16, name="w2_first", align_bytes=64), [0])
        quantise_w2(nc.scalar.copy, placed("w2_second", [P, 4 * PASS], BF16, 4), [1])
        quantise_w2(nc.scalar.copy, placed("w2_third", [P, 4 * PASS], BF16, 20), [2])
        quantise_w2(nc.scalar.copy, placed("w2_fourth", [P, 4 * PASS], BF16, 24), [3])
        for i in range(TILES):
            g, t = divmod(i, PACK)
            feat = feats[i][0]
            cols = slice(P * (i % 2), P * (i % 2 + 1))
            if i == 0:
                page = first_page
            else:
                page = placed("page%d" % i, [P, S], F32, (0, 8, 30, 34)[i % 4])
                nc.scalar.activation(page[:], feat[:], ACT.Copy, scale=gain_skip[:, g, t : t + 1])
            worked = placed("worked%d" % i, [P, M], F32, (32, 34, 40, 42, 44, 46, 38, 16)[i])
            acc = psum.tile([P, M], F32, name="acc_worked")
            for a in range(GROUPS):
                codes, scales = w2_q[i // 2, a]
                nc.tensor.matmul_mx(
                    out=acc[:],
                    lhsT=codes[:, cols].bitcast(FP8X4),
                    lhsT_scale=scales[:, cols],
                    rhs=x_q[a][0][:].bitcast(FP8X4),
                    rhs_scale=x_q[a][1][:],
                    start=(a == 0),
                    stop=(a == GROUPS - 1),
                )
            nc.scalar.activation(worked[:], acc[:], ACT.Tanh)
            engine = nc.vector if i == 0 else nc.gpsimd
            weight = weights[min(i, 1)]
            engine.tensor_tensor(weight[:], absorb_sb[g][:, t, :], wgo_sb[:, t, :], MULT)
            engine.tensor_tensor(worked[:], worked[:], weight[:], MULT)
            nc.vector.tensor_copy(page[:].indirect(pos_sb[:]), worked[:])
            nc.sync.dma_start(out=out_rows[g, t], in_=page[:])
